import numpy as np, ml_dtypes
CORES = [51,54,179,182]
N = 4
import mx_ref
NC = 128
BF = ml_dtypes.bfloat16
def cut(t, i, w=512):
    return t[:, w * i:w * i + w]
def tile(rs):
    return np.stack(rs, axis=2).reshape(128, -1).astype(BF)
def onehot(t, r):
    own, p, b = t[:, :NC], t[:, NC:2 * NC], t[:, 2 * NC:]
    return tile([((own == r) & (p == np.arange(128)[:, None]) & (b == f)).astype(np.float32) for f in range(4)])
def setup_inputs(rng):
    def f(*shape):
        return mx_ref.flush((rng.standard_normal(shape, dtype=np.float32) * np.exp2(rng.integers(-2, 3, shape[:-1] + (1,)))).astype(BF))
    t = np.concatenate([rng.integers(0, N, (N, 1, NC)), rng.integers(0, 128, (N, 1, NC)), rng.integers(0, 4, (N, 1, NC))], axis=2)
    return {"tg": np.broadcast_to(t, (N, 128, 3 * NC)).astype(BF).copy(), "tab": f(N, 128, 4 * 512), "w": f(N, 128, 512)}
def setup_inputs_blocks(rng):
    d = setup_inputs(rng)
    for k in ("tab", "w"): d[k] = mx_ref.spread(d[k], rng, 4)
    return d
def setup_inputs_wide(rng):
    d = setup_inputs(rng)
    for k in ("tab", "w"): d[k] = mx_ref.flush((d[k].astype(np.float32) * np.exp2(rng.integers(-6, 7, (N, 1, 1))).astype(np.float32)).astype(BF))
    return d
def setup_inputs_hot(rng):
    d = setup_inputs(rng); t = d["tg"].astype(np.float32); t[:, :, :NC] = rng.integers(0, N); t[:, :, NC:2 * NC] = np.broadcast_to(rng.integers(0, 4, (N, 1, NC)), (N, 128, NC))
    d["tg"] = t.astype(BF)
    return d
def reference(tg, tab, w):
    y = np.zeros((N, 128, NC), np.float32)
    for j in range(N):
        qw = mx_ref.quantize(w[j])
        for r in range(N):
            o = mx_ref.quantize(onehot(tg[j].astype(np.float32), r))
            e = mx_ref.quantize(tile([mx_ref.matmul(mx_ref.quantize(cut(tab[r], f)), o) for f in range(4)]))
            p = mx_ref.matmul(qw, e)
            y[j] = p if r == 0 else y[j] + p
    return {"y": y}

@@ -1,0 +1,246 @@
+from concourse.bass import DstId, RemoteDMATransfer
+from concourse.mybir import dt, AluOpType, ActivationFunctionType
+
+ROLES = ("S", "A", "B", "M")
+NB = 4
+
+SCRATCH = {
+    "ids": ("sbuf", [128, 24], "bfloat16"),
+    "enc": ("sbuf", [128, 16], "float32"),
+    "kA": ("sbuf", [128, 4], "bfloat16"),
+    "kB": ("sbuf", [128, 4], "bfloat16"),
+    "rS": ("sbuf", [128, 4], "bfloat16"),
+    "kM": ("sbuf", [128, 1], "bfloat16"),
+    "rA": ("sbuf", [128, 4], "bfloat16"),
+    "rB": ("sbuf", [128, 4], "bfloat16"),
+    "rM": ("sbuf", [128, 4], "bfloat16"),
+    "dM": ("dram", [128, 1], "bfloat16"),
+    "zero": ("sbuf", [128, 32], "bfloat16"),
+    "ref": ("sbuf", [128, 4], "bfloat16"),
+    "tab_s": ("sbuf", [128, 2048], "bfloat16"),
+    "w_s": ("sbuf", [128, 512], "bfloat16"),
+    "qt": ("sbuf", [128, 512], "float8_e4m3fn_x4"),
+    "st": ("sbuf", [128, 512], "uint8"),
+    "qw": ("sbuf", [128, 128], "float8_e4m3fn_x4"),
+    "sw": ("sbuf", [128, 128], "uint8"),
+    "ysb": ("sbuf", [128, 128], "float32"),
+    "p0": ("psum", [128, 2048], "float32"),
+    "p1": ("psum", [128, 2048], "float32"),
+}
+for _x in ROLES:
+    SCRATCH["bc" + _x] = ("sbuf", [128, 128], "bfloat16")
+    SCRATCH["kb" + _x] = ("sbuf", [128, 128], "bfloat16")
+    SCRATCH["o" + _x] = ("sbuf", [128, 512], "bfloat16")
+    SCRATCH["e" + _x] = ("sbuf", [128, 512], "bfloat16")
+    SCRATCH["qo" + _x] = ("sbuf", [128, 128], "float8_e4m3fn_x4")
+    SCRATCH["so" + _x] = ("sbuf", [128, 128], "uint8")
+    SCRATCH["qe" + _x] = ("sbuf", [128, 128], "float8_e4m3fn_x4")
+    SCRATCH["se" + _x] = ("sbuf", [128, 128], "uint8")
+    if _x != "S":
+        SCRATCH["lc" + _x] = ("sbuf", [128, 128], "float8_e4m3fn_x4")
+        SCRATCH["lp" + _x] = ("sbuf", [128, 128], "uint8")
+
+SEMAPHORES = ["l_p", "l_b", "l_o", "l_t0", "l_t1", "l_w", "l_m", "ref", "zero", "t1", "t2", "t3", "u", "kAB", "kM", "kS",
+              "iA", "iB", "iM", "qt0", "qt1", "qt2", "qt3", "qw", "aA", "aB", "aM", "sent", "my", "yc", "l_y"]
+for _x in ROLES:
+    SEMAPHORES += ["bc" + _x, "tr" + _x, "cm" + _x, "qo" + _x, "ev" + _x, "qe" + _x] + ["mm%s%d" % (_x, _f) for _f in range(4)]
+
+
+def engines(mask):
+    return [i for i in range(mask.bit_length()) if (mask >> i) & 1]
+
+
+def bits(lst):
+    return sum(1 << i for i in lst)
+
+
+def rank_program(g, core, T, topo):
+    rank = T.rank_of(core)
+    if rank is None:
+        return
+    S = T.sem
+    V, A, P, Y = g.vector, g.scalar, g.tensor, g.sync
+    OP, FN = AluOpType, ActivationFunctionType
+
+    peer = {}
+    for c in T.cores:
+        if c == core:
+            continue
+        if topo.host(c) == topo.host(core) and topo.chip(c) == topo.chip(core):
+            peer["M"] = c
+        elif topo.die(c) == topo.die(core):
+            peer["A"] = c
+        else:
+            peer["B"] = c
+    offchip = [i for i in engines(topo.mask(core, peer["A"])) if i in engines(topo.mask(core, peer["B"]))]
+    half = len(offchip) // 2
+    eng = {"A": offchip[:half], "B": offchip[half:],
+           "M": [i for i in engines(topo.mask(core, peer["M"])) if i not in offchip]}
+    number = {x: T.rank_of(c) for x, c in peer.items()}
+    number["S"] = rank
+    landing = {x: len(eng[x]) for x in eng}
+    sent = [0]
+
+    def fused(items, sem):
+        trs = []
+        for x, dst, src in items:
+            rid, pid = topo.addr(peer[x], core)
+            trs.append(RemoteDMATransfer(dst_ids=[DstId(rid=rid, pnc=pid)], dma_engine_mask=bits(eng[x]),
+                                         remote_sem=S[sem + x], src=src, dst=dst))
+            sent[0] += len(eng[x])
+        g.remote_dma_fused(trs, local_sem=S["sent"])
+
+    def single(x, dst, src, sem):
+        rid, pid = topo.addr(peer[x], core)
+        g.remote_dma(out_ap=dst, in_ap=src, remote_sem=S[sem + x], local_sem=S["sent"], pid=pid, routing_id=rid,
+                     dma_engine_mask=bits(eng[x]))
+        sent[0] += len(eng[x])
+
+    def codes(name):
+        return T[name][:].bitcast(dt.uint8)
+
+    Y.dma_start(T.ids[:, 16:20], T.tg[0:4, 0:128]).then_inc(S["l_o"], 16)
+    A.dma_start(T.ids[:, 0:4], T.tg[0:4, 128:256]).then_inc(S["l_p"], 16)
+    Y.dma_start(T.ids[:, 8:12], T.tg[0:4, 256:384]).then_inc(S["l_b"], 16)
+    A.dma_start(T.tab_s[:, 0:1024], T.tab[:, 0:1024]).then_inc(S["l_t0"], 16)
+    Y.dma_start(T.tab_s[:, 1024:2048], T.tab[:, 1024:2048]).then_inc(S["l_t1"], 16)
+    Y.dma_start(T.w_s[:], T.w[:]).then_inc(S["l_w"], 16)
+
+    g.iota(T.ref[:], [[1, NB]], -256, NB, allow_small_or_imprecise_dtypes=True).then_inc(S["ref"], 1)
+    g.wait_ge(S["kAB"], 2)
+    fused([("A", T.rA[:], T.kA[:]), ("B", T.rB[:], T.kB[:])], "i")
+    g.wait_ge(S["kM"], 4)
+    single("M", T.dM[:], T.kM[:], "i")
+    g.wait_ge(S["qeA"], 1)
+    g.wait_ge(S["qeB"], 1)
+    fused([("A", codes("lcA"), codes("qeA")), ("B", codes("lcB"), codes("qeB"))], "a")
+    fused([("A", T.lpA[:], T.seA[:]), ("B", T.lpB[:], T.seB[:])], "a")
+    g.wait_ge(S["qeM"], 1)
+    single("M", codes("lcM"), codes("qeM"), "a")
+    single("M", T.lpM[:], T.seM[:], "a")
+    g.wait_ge(S["sent"], sent[0])
+
+    Y.wait_ge(S["iM"], landing["M"])
+    for a in range(4):
+        Y.dma_start(T.rM[32 * a:32 * a + 32, :], T.dM[:]).then_inc(S["l_m"], 16)
+    Y.wait_ge(S["yc"], 4)
+    Y.dma_start(T.y[:], T.ysb[:]).then_inc(S["l_y"], 16)
+    Y.wait_ge(S["l_y"], 16)
+
+    arrival = {"S": ("kS", 1), "A": ("iA", landing["A"]), "B": ("iB", landing["B"]), "M": ("l_m", 64)}
+    psum = {"S": T.p0, "A": T.p1, "B": T.p0, "M": T.p1}
+
+    def spread(queue, x, cols):
+        queue.wait_ge(S[arrival[x][0]], arrival[x][1])
+        for B in cols:
+            out, key = T["bc" + x][:, 32 * B:32 * B + 32], T["r" + x][:, B:B + 1]
+            if queue is A:
+                A.activation(out, T.zero[:], FN.Identity, bias=key).then_inc(S["bc" + x], 1)
+            else:
+                V.tensor_scalar(out, T.zero[:], key, None, OP.add).then_inc(S["bc" + x], 1)
+
+    def onehot(x):
+        V.wait_ge(S["bc" + x], 4)
+        if x == "M":
+            for B in range(4):
+                V.transpose(T.kbM[:, B:128:4], T.bcM[:, 32 * B:32 * B + 32]).then_inc(S["trM"], 1)
+            V.wait_ge(S["trM"], 4)
+        else:
+            V.transpose(T["kb" + x][:], T["bc" + x][:]).then_inc(S["tr" + x], 1)
+            V.wait_ge(S["tr" + x], 1)
+        for b in range(NB):
+            V.tensor_scalar(T["o" + x][:, b:512:4], T["kb" + x][:], T.ref[:, b:b + 1], None, OP.is_equal).then_inc(S["cm" + x], 1)
+        V.wait_ge(S["cm" + x], 4)
+        V.quantize_mx(T["qo" + x][:], T["so" + x][:], T["o" + x][:]).then_inc(S["qo" + x], 1)
+
+    def evacuate(queue, x, fs):
+        for f in fs:
+            queue.wait_ge(S["mm%s%d" % (x, f)], 1)
+            out, src = T["e" + x][:, f:512:4], psum[x][:, 512 * f:512 * f + 128]
+            if queue is A:
+                A.activation(out, src, FN.Copy).then_inc(S["ev" + x], 1)
+            else:
+                V.tensor_copy(out, src).then_inc(S["ev" + x], 1)
+
+    def quantise_entry(x):
+        V.wait_ge(S["ev" + x], 4)
+        V.quantize_mx(T["qe" + x][:], T["se" + x][:], T["e" + x][:]).then_inc(S["qe" + x], 1)
+
+    V.memset(T.zero[:], 0.0).then_inc(S["zero"], 1)
+    V.wait_ge(S["l_o"], 16)
+    V.tensor_scalar(T.enc[:, 0:4], T.ids[:, 16:20], 1024.0, -256.0, OP.mult, OP.add).then_inc(S["t1"], 1)
+    V.wait_ge(S["l_b"], 16)
+    V.wait_ge(S["t1"], 1)
+    V.tensor_tensor(T.enc[:, 8:12], T.enc[:, 0:4], T.ids[:, 8:12], OP.add).then_inc(S["t3"], 1)
+    V.wait_ge(S["t2"], 1)
+    V.wait_ge(S["t3"], 1)
+    V.tensor_tensor(T.enc[:, 12:16], T.enc[:, 8:12], T.enc[:, 4:8], OP.add).then_inc(S["u"], 1)
+    V.wait_ge(S["u"], 1)
+    for x in ("A", "B"):
+        V.tensor_scalar(T["k" + x][:], T.enc[:, 12:16], -1024.0 * number[x], None, OP.add).then_inc(S["kAB"], 1)
+    for a in range(4):
+        V.tensor_scalar(T.kM[32 * a:32 * a + 32, 0:1], T.enc[32 * a:32 * a + 32, 12 + a:13 + a], -1024.0 * number["M"], None,
+                        OP.add).then_inc(S["kM"], 1)
+    V.tensor_scalar(T.rS[:], T.enc[:, 12:16], -1024.0 * rank, None, OP.add).then_inc(S["kS"], 1)
+    V.wait_ge(S["zero"], 1)
+    V.wait_ge(S["ref"], 1)
+    spread(V, "S", (0, 1))
+    onehot("S")
+    for f in range(4):
+        if f % 2 == 0:
+            V.wait_ge(S["l_t%d" % (f // 2)], 16)
+        V.quantize_mx(T.qt[:, 128 * f:128 * f + 128], T.st[:, 128 * f:128 * f + 128],
+                      T.tab_s[:, 512 * f:512 * f + 512]).then_inc(S["qt%d" % f], 1)
+    for x in ("A", "B"):
+        spread(V, x, (0, 1))
+        onehot(x)
+    for x in ("A", "B"):
+        evacuate(V, x, (1, 3))
+        quantise_entry(x)
+    spread(V, "M", (0, 1))
+    onehot("M")
+    V.wait_ge(S["l_w"], 16)
+    V.quantize_mx(T.qw[:], T.sw[:], T.w_s[:]).then_inc(S["qw"], 1)
+    quantise_entry("S")
+    evacuate(V, "M", (1, 3))
+    quantise_entry("M")
+    V.wait_ge(S["my"], 1)
+    for B in range(4):
+        V.tensor_copy(T.ysb[:, B:128:4], T.p0[:, 32 * B:32 * B + 32]).then_inc(S["yc"], 1)
+
+    A.wait_ge(S["l_p"], 16)
+    A.activation(T.enc[:, 4:8], T.ids[:, 0:4], FN.Copy, scale=4.0).then_inc(S["t2"], 1)
+    A.wait_ge(S["zero"], 1)
+    spread(A, "S", (2, 3))
+    evacuate(A, "S", (0, 1, 2, 3))
+    for x in ("A", "B"):
+        spread(A, x, (2, 3))
+    for x in ("A", "B"):
+        evacuate(A, x, (0, 2))
+    spread(A, "M", (2, 3))
+    evacuate(A, "M", (0, 2))
+
+    for x in ROLES:
+        P.wait_ge(S["qo" + x], 1)
+        if x == "B":
+            P.wait_ge(S["evS"], 4)
+        if x == "M":
+            P.wait_ge(S["evA"], 4)
+        for f in range(4):
+            if x == "S":
+                P.wait_ge(S["qt%d" % f], 1)
+            P.matmul_mx(psum[x][:, 512 * f:512 * f + 128], T.qt[:, 128 * f:128 * f + 128], T.st[:, 128 * f:128 * f + 128],
+                        T["qo" + x][:], T["so" + x][:], True, True).then_inc(S["mm%s%d" % (x, f)], 1)
+    P.wait_ge(S["evB"], 4)
+    P.wait_ge(S["qw"], 1)
+    P.wait_ge(S["qeS"], 1)
+    order = ("S", "M", "A", "B")
+    for i, x in enumerate(order):
+        if x == "S":
+            c, s = T.qeS, T.seS
+        else:
+            P.wait_ge(S["a" + x], 2 * landing[x])
+            c, s = T["lc" + x], T["lp" + x]
+        mm = P.matmul_mx(T.p0[:, 0:128], T.qw[:], T.sw[:], c[:], s[:], i == 0, i == 3)
+        if i == 3:
+            mm.then_inc(S["my"], 1)

@@ -6,14 +6,9 @@ NB = 4
 
 SCRATCH = {
     "ids": ("sbuf", [128, 24], "bfloat16"),
-    "enc": ("sbuf", [128, 16], "float32"),
-    "kA": ("sbuf", [128, 4], "bfloat16"),
-    "kB": ("sbuf", [128, 4], "bfloat16"),
-    "rS": ("sbuf", [128, 4], "bfloat16"),
+    "p4": ("sbuf", [128, 4], "float32"),
+    "en": ("sbuf", [128, 4], "float32"),
     "kM": ("sbuf", [128, 1], "bfloat16"),
-    "rA": ("sbuf", [128, 4], "bfloat16"),
-    "rB": ("sbuf", [128, 4], "bfloat16"),
-    "rM": ("sbuf", [128, 4], "bfloat16"),
     "dM": ("dram", [128, 1], "bfloat16"),
     "zero": ("sbuf", [128, 32], "bfloat16"),
     "ref": ("sbuf", [128, 4], "bfloat16"),
@@ -28,6 +23,7 @@ SCRATCH = {
     "p1": ("psum", [128, 2048], "float32"),
 }
 for _x in ROLES:
+    SCRATCH["r" + _x] = ("sbuf", [128, 4], "bfloat16")
     SCRATCH["bc" + _x] = ("sbuf", [128, 128], "bfloat16")
     SCRATCH["kb" + _x] = ("sbuf", [128, 128], "bfloat16")
     SCRATCH["o" + _x] = ("sbuf", [128, 512], "bfloat16")
@@ -39,11 +35,15 @@ for _x in ROLES:
     if _x != "S":
         SCRATCH["lc" + _x] = ("sbuf", [128, 128], "float8_e4m3fn_x4")
         SCRATCH["lp" + _x] = ("sbuf", [128, 128], "uint8")
+for _x in ("A", "B"):
+    SCRATCH["k" + _x] = ("sbuf", [128, 4], "bfloat16")
+SCRATCH["ow"] = ("sbuf", [128, 64], "float32")
 
-SEMAPHORES = ["l_p", "l_b", "l_o", "l_t0", "l_t1", "l_w", "l_m", "ref", "zero", "t1", "t2", "t3", "u", "kAB", "kM", "kS",
-              "iA", "iB", "iM", "qt0", "qt1", "qt2", "qt3", "qw", "aA", "aB", "aM", "sent", "my", "yc", "l_y"]
+SEMAPHORES = ["l_p", "l_b", "l_o", "l_t0", "l_t1", "l_w", "l_m", "ref", "zero", "p4", "en", "kAB", "kM", "kS",
+              "iA", "iB", "iM", "qt0", "qt1", "qt2", "qt3", "qw", "aA", "aB", "aM", "sent", "left", "my", "yc", "l_y"]
 for _x in ROLES:
-    SEMAPHORES += ["bc" + _x, "tr" + _x, "cm" + _x, "qo" + _x, "ev" + _x, "qe" + _x] + ["mm%s%d" % (_x, _f) for _f in range(4)]
+    SEMAPHORES += ["ow" + _x, "bc" + _x, "tr" + _x, "cm" + _x, "qo" + _x, "ev" + _x, "qe" + _x]
+    SEMAPHORES += ["mm%s%d" % (_x, _f) for _f in range(4)]
 
 
 def engines(mask):
@@ -72,63 +72,65 @@ def rank_program(g, core, T, topo):
             peer["A"] = c
         else:
             peer["B"] = c
-    offchip = [i for i in engines(topo.mask(core, peer["A"])) if i in engines(topo.mask(core, peer["B"]))]
-    half = len(offchip) // 2
-    eng = {"A": offchip[:half], "B": offchip[half:],
-           "M": [i for i in engines(topo.mask(core, peer["M"])) if i not in offchip]}
+    off = [i for i in engines(topo.mask(core, peer["A"])) if i in engines(topo.mask(core, peer["B"]))]
+    on = [i for i in engines(topo.mask(core, peer["M"])) if i not in off]
+    half = {"A": off[:len(off) // 2], "B": off[len(off) // 2:]}
     number = {x: T.rank_of(c) for x, c in peer.items()}
     number["S"] = rank
-    landing = {x: len(eng[x]) for x in eng}
-    sent = [0]
+    sent = {"sent": 0, "left": 0}
 
-    def fused(items, sem):
+    def send(items, sem, local="sent"):
         trs = []
-        for x, dst, src in items:
+        for x, dst, src, es in items:
             rid, pid = topo.addr(peer[x], core)
-            trs.append(RemoteDMATransfer(dst_ids=[DstId(rid=rid, pnc=pid)], dma_engine_mask=bits(eng[x]),
+            trs.append(RemoteDMATransfer(dst_ids=[DstId(rid=rid, pnc=pid)], dma_engine_mask=bits(es),
                                          remote_sem=S[sem + x], src=src, dst=dst))
-            sent[0] += len(eng[x])
-        g.remote_dma_fused(trs, local_sem=S["sent"])
-
-    def single(x, dst, src, sem):
-        rid, pid = topo.addr(peer[x], core)
-        g.remote_dma(out_ap=dst, in_ap=src, remote_sem=S[sem + x], local_sem=S["sent"], pid=pid, routing_id=rid,
-                     dma_engine_mask=bits(eng[x]))
-        sent[0] += len(eng[x])
+            sent[local] += len(es)
+        g.remote_dma_fused(trs, local_sem=S[local])
 
     def codes(name):
         return T[name][:].bitcast(dt.uint8)
 
-    Y.dma_start(T.ids[:, 16:20], T.tg[0:4, 0:128]).then_inc(S["l_o"], 16)
-    A.dma_start(T.ids[:, 0:4], T.tg[0:4, 128:256]).then_inc(S["l_p"], 16)
-    Y.dma_start(T.ids[:, 8:12], T.tg[0:4, 256:384]).then_inc(S["l_b"], 16)
-    A.dma_start(T.tab_s[:, 0:1024], T.tab[:, 0:1024]).then_inc(S["l_t0"], 16)
-    Y.dma_start(T.tab_s[:, 1024:2048], T.tab[:, 1024:2048]).then_inc(S["l_t1"], 16)
-    Y.dma_start(T.w_s[:], T.w[:]).then_inc(S["l_w"], 16)
+    ids_in = {"A": len(half["A"]), "B": len(half["B"]), "M": len(on)}
+    entries_in = {"A": len(off) + len(half["A"]), "B": len(off) + len(half["B"]), "M": 2 * len(on)}
 
     g.iota(T.ref[:], [[1, NB]], -256, NB, allow_small_or_imprecise_dtypes=True).then_inc(S["ref"], 1)
     g.wait_ge(S["kAB"], 2)
-    fused([("A", T.rA[:], T.kA[:]), ("B", T.rB[:], T.kB[:])], "i")
+    send([("A", T.rA[:], T.kA[:], half["A"]), ("B", T.rB[:], T.kB[:], half["B"])], "i", "left")
     g.wait_ge(S["kM"], 4)
-    single("M", T.dM[:], T.kM[:], "i")
-    g.wait_ge(S["qeA"], 1)
-    g.wait_ge(S["qeB"], 1)
-    fused([("A", codes("lcA"), codes("qeA")), ("B", codes("lcB"), codes("qeB"))], "a")
-    fused([("A", T.lpA[:], T.seA[:]), ("B", T.lpB[:], T.seB[:])], "a")
+    send([("M", T.dM[:], T.kM[:], on)], "i")
+    for x in ("A", "B"):
+        g.wait_ge(S["qe" + x], 1)
+        send([(x, codes("lc" + x), codes("qe" + x), off)], "a")
+    send([(x, T["lp" + x][:], T["se" + x][:], half[x]) for x in ("A", "B")], "a")
     g.wait_ge(S["qeM"], 1)
-    single("M", codes("lcM"), codes("qeM"), "a")
-    single("M", T.lpM[:], T.seM[:], "a")
-    g.wait_ge(S["sent"], sent[0])
+    send([("M", codes("lcM"), codes("qeM"), on)], "a")
+    send([("M", T.lpM[:], T.seM[:], on)], "a")
+    g.wait_ge(S["sent"], sent["sent"])
 
-    Y.wait_ge(S["iM"], landing["M"])
+    Y.dma_start(T.ids[:, 8:12], T.tg[0:4, 256:384]).then_inc(S["l_b"], 16)
+    Y.dma_start(T.ids[:, 16:20], T.tg[0:4, 0:128]).then_inc(S["l_o"], 16)
+    Y.dma_start(T.tab_s[:, 0:1024], T.tab[:, 0:1024]).then_inc(S["l_t0"], 16)
+    Y.dma_start(T.tab_s[:, 1024:2048], T.tab[:, 1024:2048]).then_inc(S["l_t1"], 16)
+    Y.wait_ge(S["left"], sent["left"])
+    Y.dma_start(T.w_s[:], T.w[:]).then_inc(S["l_w"], 16)
+    Y.wait_ge(S["iM"], ids_in["M"])
     for a in range(4):
         Y.dma_start(T.rM[32 * a:32 * a + 32, :], T.dM[:]).then_inc(S["l_m"], 16)
     Y.wait_ge(S["yc"], 4)
     Y.dma_start(T.y[:], T.ysb[:]).then_inc(S["l_y"], 16)
     Y.wait_ge(S["l_y"], 16)
 
-    arrival = {"S": ("kS", 1), "A": ("iA", landing["A"]), "B": ("iB", landing["B"]), "M": ("l_m", 64)}
+    arrival = {"S": ("kS", 1), "A": ("iA", ids_in["A"]), "B": ("iB", ids_in["B"]), "M": ("l_m", 64)}
     psum = {"S": T.p0, "A": T.p1, "B": T.p0, "M": T.p1}
+
+    def base(queue, x):
+        k, c = 16 * ROLES.index(x), -1024.0 * number[x] - 256.0
+        out, own = T.ow[:, k:k + 4], T.ids[:, 16:20]
+        if queue is A:
+            A.activation(out, own, FN.Copy, scale=1024.0, bias=c).then_inc(S["ow" + x], 1)
+        else:
+            V.tensor_scalar(out, own, 1024.0, c, OP.mult, OP.add).then_inc(S["ow" + x], 1)
 
     def spread(queue, x, cols):
         queue.wait_ge(S[arrival[x][0]], arrival[x][1])
@@ -139,17 +141,20 @@ def rank_program(g, core, T, topo):
             else:
                 V.tensor_scalar(out, T.zero[:], key, None, OP.add).then_inc(S["bc" + x], 1)
 
-    def onehot(x):
+    def turn(x):
         V.wait_ge(S["bc" + x], 4)
         if x == "M":
             for B in range(4):
                 V.transpose(T.kbM[:, B:128:4], T.bcM[:, 32 * B:32 * B + 32]).then_inc(S["trM"], 1)
-            V.wait_ge(S["trM"], 4)
         else:
             V.transpose(T["kb" + x][:], T["bc" + x][:]).then_inc(S["tr" + x], 1)
-            V.wait_ge(S["tr" + x], 1)
+
+    def compare(x):
+        V.wait_ge(S["tr" + x], 4 if x == "M" else 1)
         for b in range(NB):
             V.tensor_scalar(T["o" + x][:, b:512:4], T["kb" + x][:], T.ref[:, b:b + 1], None, OP.is_equal).then_inc(S["cm" + x], 1)
+
+    def quantise_onehot(x):
         V.wait_ge(S["cm" + x], 4)
         V.quantize_mx(T["qo" + x][:], T["so" + x][:], T["o" + x][:]).then_inc(S["qo" + x], 1)
 
@@ -166,59 +171,72 @@ def rank_program(g, core, T, topo):
         V.wait_ge(S["ev" + x], 4)
         V.quantize_mx(T["qe" + x][:], T["se" + x][:], T["e" + x][:]).then_inc(S["qe" + x], 1)
 
+    A.dma_start(T.ids[:, 0:4], T.tg[0:4, 128:256]).then_inc(S["l_p"], 16)
+    A.wait_ge(S["l_p"], 16)
+    A.activation(T.p4[:], T.ids[:, 0:4], FN.Copy, scale=4.0).then_inc(S["p4"], 1)
+    A.wait_ge(S["l_o"], 16)
+    for x in ("B", "M", "S"):
+        base(A, x)
+    A.wait_ge(S["zero"], 1)
+    spread(A, "S", (2, 3))
+    evacuate(A, "S", (0, 1, 2, 3))
+    spread(A, "A", (2, 3))
+    spread(A, "B", (0, 1, 2, 3))
+    evacuate(A, "A", (0, 1, 2))
+    spread(A, "M", (0, 1, 2, 3))
+    evacuate(A, "B", (0, 1, 2, 3))
+    evacuate(A, "M", (0, 2))
+
     V.memset(T.zero[:], 0.0).then_inc(S["zero"], 1)
-    V.wait_ge(S["l_o"], 16)
-    V.tensor_scalar(T.enc[:, 0:4], T.ids[:, 16:20], 1024.0, -256.0, OP.mult, OP.add).then_inc(S["t1"], 1)
     V.wait_ge(S["l_b"], 16)
-    V.wait_ge(S["t1"], 1)
-    V.tensor_tensor(T.enc[:, 8:12], T.enc[:, 0:4], T.ids[:, 8:12], OP.add).then_inc(S["t3"], 1)
-    V.wait_ge(S["t2"], 1)
-    V.wait_ge(S["t3"], 1)
-    V.tensor_tensor(T.enc[:, 12:16], T.enc[:, 8:12], T.enc[:, 4:8], OP.add).then_inc(S["u"], 1)
-    V.wait_ge(S["u"], 1)
+    V.wait_ge(S["p4"], 1)
+    V.tensor_tensor(T.en[:], T.p4[:], T.ids[:, 8:12], OP.add).then_inc(S["en"], 1)
+    V.wait_ge(S["l_o"], 16)
+    base(V, "A")
+    V.wait_ge(S["en"], 1)
     for x in ("A", "B"):
-        V.tensor_scalar(T["k" + x][:], T.enc[:, 12:16], -1024.0 * number[x], None, OP.add).then_inc(S["kAB"], 1)
+        k = 16 * ROLES.index(x)
+        V.wait_ge(S["ow" + x], 1)
+        V.tensor_tensor(T["k" + x][:], T.ow[:, k:k + 4], T.en[:], OP.add).then_inc(S["kAB"], 1)
+    V.wait_ge(S["owM"], 1)
+    k = 16 * ROLES.index("M")
     for a in range(4):
-        V.tensor_scalar(T.kM[32 * a:32 * a + 32, 0:1], T.enc[32 * a:32 * a + 32, 12 + a:13 + a], -1024.0 * number["M"], None,
-                        OP.add).then_inc(S["kM"], 1)
-    V.tensor_scalar(T.rS[:], T.enc[:, 12:16], -1024.0 * rank, None, OP.add).then_inc(S["kS"], 1)
+        V.tensor_tensor(T.kM[32 * a:32 * a + 32, 0:1], T.ow[32 * a:32 * a + 32, k + a:k + a + 1],
+                        T.en[32 * a:32 * a + 32, a:a + 1], OP.add).then_inc(S["kM"], 1)
+    V.wait_ge(S["owS"], 1)
+    V.tensor_tensor(T.rS[:], T.ow[:, 0:4], T.en[:], OP.add).then_inc(S["kS"], 1)
     V.wait_ge(S["zero"], 1)
     V.wait_ge(S["ref"], 1)
     spread(V, "S", (0, 1))
-    onehot("S")
+    turn("S")
+    compare("S")
+    quantise_onehot("S")
     for f in range(4):
         if f % 2 == 0:
             V.wait_ge(S["l_t%d" % (f // 2)], 16)
         V.quantize_mx(T.qt[:, 128 * f:128 * f + 128], T.st[:, 128 * f:128 * f + 128],
                       T.tab_s[:, 512 * f:512 * f + 512]).then_inc(S["qt%d" % f], 1)
-    for x in ("A", "B"):
-        spread(V, x, (0, 1))
-        onehot(x)
-    for x in ("A", "B"):
-        evacuate(V, x, (1, 3))
-        quantise_entry(x)
-    spread(V, "M", (0, 1))
-    onehot("M")
+    quantise_entry("S")
+    spread(V, "A", (0, 1))
+    turn("A")
+    compare("A")
+    turn("B")
+    quantise_onehot("A")
+    compare("B")
+    quantise_onehot("B")
+    evacuate(V, "A", (3,))
+    quantise_entry("A")
+    turn("M")
+    compare("M")
+    quantise_onehot("M")
+    quantise_entry("B")
     V.wait_ge(S["l_w"], 16)
     V.quantize_mx(T.qw[:], T.sw[:], T.w_s[:]).then_inc(S["qw"], 1)
-    quantise_entry("S")
     evacuate(V, "M", (1, 3))
     quantise_entry("M")
     V.wait_ge(S["my"], 1)
     for B in range(4):
         V.tensor_copy(T.ysb[:, B:128:4], T.p0[:, 32 * B:32 * B + 32]).then_inc(S["yc"], 1)
-
-    A.wait_ge(S["l_p"], 16)
-    A.activation(T.enc[:, 4:8], T.ids[:, 0:4], FN.Copy, scale=4.0).then_inc(S["t2"], 1)
-    A.wait_ge(S["zero"], 1)
-    spread(A, "S", (2, 3))
-    evacuate(A, "S", (0, 1, 2, 3))
-    for x in ("A", "B"):
-        spread(A, x, (2, 3))
-    for x in ("A", "B"):
-        evacuate(A, x, (0, 2))
-    spread(A, "M", (2, 3))
-    evacuate(A, "M", (0, 2))
 
     for x in ROLES:
         P.wait_ge(S["qo" + x], 1)
@@ -234,12 +252,12 @@ def rank_program(g, core, T, topo):
     P.wait_ge(S["evB"], 4)
     P.wait_ge(S["qw"], 1)
     P.wait_ge(S["qeS"], 1)
-    order = ("S", "M", "A", "B")
+    order = ("S", "A", "B", "M")
     for i, x in enumerate(order):
         if x == "S":
             c, s = T.qeS, T.seS
         else:
-            P.wait_ge(S["a" + x], 2 * landing[x])
+            P.wait_ge(S["a" + x], entries_in[x])
             c, s = T["lc" + x], T["lp" + x]
         mm = P.matmul_mx(T.p0[:, 0:128], T.qw[:], T.sw[:], c[:], s[:], i == 0, i == 3)
         if i == 3:

from concourse.bass import DstId, RemoteDMATransfer
from concourse.mybir import dt, AluOpType, ActivationFunctionType

ROLES = ("S", "A", "B", "M")
NB = 4

SCRATCH = {
    "ids": ("sbuf", [128, 24], "bfloat16"),
    "p4": ("sbuf", [128, 4], "float32"),
    "en": ("sbuf", [128, 4], "float32"),
    "kM": ("sbuf", [128, 1], "bfloat16"),
    "dM": ("dram", [128, 1], "bfloat16"),
    "zero": ("sbuf", [128, 32], "bfloat16"),
    "ref": ("sbuf", [128, 4], "bfloat16"),
    "tab_s": ("sbuf", [128, 2048], "bfloat16"),
    "w_s": ("sbuf", [128, 512], "bfloat16"),
    "qt": ("sbuf", [128, 512], "float8_e4m3fn_x4"),
    "st": ("sbuf", [128, 512], "uint8"),
    "qw": ("sbuf", [128, 128], "float8_e4m3fn_x4"),
    "sw": ("sbuf", [128, 128], "uint8"),
    "ysb": ("sbuf", [128, 128], "float32"),
    "p0": ("psum", [128, 2048], "float32"),
    "p1": ("psum", [128, 2048], "float32"),
}
for _x in ROLES:
    SCRATCH["r" + _x] = ("sbuf", [128, 4], "bfloat16")
    SCRATCH["bc" + _x] = ("sbuf", [128, 128], "bfloat16")
    SCRATCH["kb" + _x] = ("sbuf", [128, 128], "bfloat16")
    SCRATCH["o" + _x] = ("sbuf", [128, 512], "bfloat16")
    SCRATCH["e" + _x] = ("sbuf", [128, 512], "bfloat16")
    SCRATCH["qo" + _x] = ("sbuf", [128, 128], "float8_e4m3fn_x4")
    SCRATCH["so" + _x] = ("sbuf", [128, 128], "uint8")
    SCRATCH["qe" + _x] = ("sbuf", [128, 128], "float8_e4m3fn_x4")
    SCRATCH["se" + _x] = ("sbuf", [128, 128], "uint8")
    if _x != "S":
        SCRATCH["lc" + _x] = ("sbuf", [128, 128], "float8_e4m3fn_x4")
        SCRATCH["lp" + _x] = ("sbuf", [128, 128], "uint8")
for _x in ("A", "B"):
    SCRATCH["k" + _x] = ("sbuf", [128, 4], "bfloat16")
SCRATCH["ow"] = ("sbuf", [128, 64], "float32")

SEMAPHORES = ["l_p", "l_b", "l_o", "l_t0", "l_t1", "l_w", "l_m", "ref", "zero", "p4", "en", "kAB", "kM", "kS",
              "iA", "iB", "iM", "qt0", "qt1", "qt2", "qt3", "qw", "aA", "aB", "aM", "sent", "left", "my", "yc", "l_y"]
for _x in ROLES:
    SEMAPHORES += ["ow" + _x, "bc" + _x, "tr" + _x, "cm" + _x, "qo" + _x, "ev" + _x, "qe" + _x]
    SEMAPHORES += ["mm%s%d" % (_x, _f) for _f in range(4)]


def engines(mask):
    return [i for i in range(mask.bit_length()) if (mask >> i) & 1]


def bits(lst):
    return sum(1 << i for i in lst)


def rank_program(g, core, T, topo):
    rank = T.rank_of(core)
    if rank is None:
        return
    S = T.sem
    V, A, P, Y = g.vector, g.scalar, g.tensor, g.sync
    OP, FN = AluOpType, ActivationFunctionType

    peer = {}
    for c in T.cores:
        if c == core:
            continue
        if topo.host(c) == topo.host(core) and topo.chip(c) == topo.chip(core):
            peer["M"] = c
        elif topo.die(c) == topo.die(core):
            peer["A"] = c
        else:
            peer["B"] = c
    off = [i for i in engines(topo.mask(core, peer["A"])) if i in engines(topo.mask(core, peer["B"]))]
    on = [i for i in engines(topo.mask(core, peer["M"])) if i not in off]
    half = {"A": off[:len(off) // 2], "B": off[len(off) // 2:]}
    number = {x: T.rank_of(c) for x, c in peer.items()}
    number["S"] = rank
    sent = {"sent": 0, "left": 0}

    def send(items, sem, local="sent"):
        trs = []
        for x, dst, src, es in items:
            rid, pid = topo.addr(peer[x], core)
            trs.append(RemoteDMATransfer(dst_ids=[DstId(rid=rid, pnc=pid)], dma_engine_mask=bits(es),
                                         remote_sem=S[sem + x], src=src, dst=dst))
            sent[local] += len(es)
        g.remote_dma_fused(trs, local_sem=S[local])

    def codes(name):
        return T[name][:].bitcast(dt.uint8)

    ids_in = {"A": len(half["A"]), "B": len(half["B"]), "M": len(on)}
    entries_in = {"A": len(off) + len(half["A"]), "B": len(off) + len(half["B"]), "M": 2 * len(on)}

    g.iota(T.ref[:], [[1, NB]], -256, NB, allow_small_or_imprecise_dtypes=True).then_inc(S["ref"], 1)
    g.wait_ge(S["kAB"], 2)
    send([("A", T.rA[:], T.kA[:], half["A"]), ("B", T.rB[:], T.kB[:], half["B"])], "i", "left")
    g.wait_ge(S["kM"], 4)
    send([("M", T.dM[:], T.kM[:], on)], "i")
    for x in ("A", "B"):
        g.wait_ge(S["qe" + x], 1)
        send([(x, codes("lc" + x), codes("qe" + x), off)], "a")
    send([(x, T["lp" + x][:], T["se" + x][:], half[x]) for x in ("A", "B")], "a")
    g.wait_ge(S["qeM"], 1)
    send([("M", codes("lcM"), codes("qeM"), on)], "a")
    send([("M", T.lpM[:], T.seM[:], on)], "a")
    g.wait_ge(S["sent"], sent["sent"])

    Y.dma_start(T.ids[:, 8:12], T.tg[0:4, 256:384]).then_inc(S["l_b"], 16)
    Y.dma_start(T.ids[:, 16:20], T.tg[0:4, 0:128]).then_inc(S["l_o"], 16)
    Y.dma_start(T.tab_s[:, 0:1024], T.tab[:, 0:1024]).then_inc(S["l_t0"], 16)
    Y.dma_start(T.tab_s[:, 1024:2048], T.tab[:, 1024:2048]).then_inc(S["l_t1"], 16)
    Y.wait_ge(S["left"], sent["left"])
    Y.dma_start(T.w_s[:], T.w[:]).then_inc(S["l_w"], 16)
    Y.wait_ge(S["iM"], ids_in["M"])
    for a in range(4):
        Y.dma_start(T.rM[32 * a:32 * a + 32, :], T.dM[:]).then_inc(S["l_m"], 16)
    Y.wait_ge(S["yc"], 4)
    Y.dma_start(T.y[:], T.ysb[:]).then_inc(S["l_y"], 16)
    Y.wait_ge(S["l_y"], 16)

    arrival = {"S": ("kS", 1), "A": ("iA", ids_in["A"]), "B": ("iB", ids_in["B"]), "M": ("l_m", 64)}
    psum = {"S": T.p0, "A": T.p1, "B": T.p0, "M": T.p1}

    def base(queue, x):
        k, c = 16 * ROLES.index(x), -1024.0 * number[x] - 256.0
        out, own = T.ow[:, k:k + 4], T.ids[:, 16:20]
        if queue is A:
            A.activation(out, own, FN.Copy, scale=1024.0, bias=c).then_inc(S["ow" + x], 1)
        else:
            V.tensor_scalar(out, own, 1024.0, c, OP.mult, OP.add).then_inc(S["ow" + x], 1)

    def spread(queue, x, cols):
        queue.wait_ge(S[arrival[x][0]], arrival[x][1])
        for B in cols:
            out, key = T["bc" + x][:, 32 * B:32 * B + 32], T["r" + x][:, B:B + 1]
            if queue is A:
                A.activation(out, T.zero[:], FN.Identity, bias=key).then_inc(S["bc" + x], 1)
            else:
                V.tensor_scalar(out, T.zero[:], key, None, OP.add).then_inc(S["bc" + x], 1)

    def turn(x):
        V.wait_ge(S["bc" + x], 4)
        if x == "M":
            for B in range(4):
                V.transpose(T.kbM[:, B:128:4], T.bcM[:, 32 * B:32 * B + 32]).then_inc(S["trM"], 1)
        else:
            V.transpose(T["kb" + x][:], T["bc" + x][:]).then_inc(S["tr" + x], 1)

    def compare(x):
        V.wait_ge(S["tr" + x], 4 if x == "M" else 1)
        for b in range(NB):
            V.tensor_scalar(T["o" + x][:, b:512:4], T["kb" + x][:], T.ref[:, b:b + 1], None, OP.is_equal).then_inc(S["cm" + x], 1)

    def quantise_onehot(x):
        V.wait_ge(S["cm" + x], 4)
        V.quantize_mx(T["qo" + x][:], T["so" + x][:], T["o" + x][:]).then_inc(S["qo" + x], 1)

    def evacuate(queue, x, fs):
        for f in fs:
            queue.wait_ge(S["mm%s%d" % (x, f)], 1)
            out, src = T["e" + x][:, f:512:4], psum[x][:, 512 * f:512 * f + 128]
            if queue is A:
                A.activation(out, src, FN.Copy).then_inc(S["ev" + x], 1)
            else:
                V.tensor_copy(out, src).then_inc(S["ev" + x], 1)

    def quantise_entry(x):
        V.wait_ge(S["ev" + x], 4)
        V.quantize_mx(T["qe" + x][:], T["se" + x][:], T["e" + x][:]).then_inc(S["qe" + x], 1)

    A.dma_start(T.ids[:, 0:4], T.tg[0:4, 128:256]).then_inc(S["l_p"], 16)
    A.wait_ge(S["l_p"], 16)
    A.activation(T.p4[:], T.ids[:, 0:4], FN.Copy, scale=4.0).then_inc(S["p4"], 1)
    A.wait_ge(S["l_o"], 16)
    for x in ("B", "M", "S"):
        base(A, x)
    A.wait_ge(S["zero"], 1)
    spread(A, "S", (2, 3))
    evacuate(A, "S", (0, 1, 2, 3))
    spread(A, "A", (2, 3))
    spread(A, "B", (0, 1, 2, 3))
    evacuate(A, "A", (0, 1, 2))
    spread(A, "M", (0, 1, 2, 3))
    evacuate(A, "B", (0, 1, 2, 3))
    evacuate(A, "M", (0, 2))

    V.memset(T.zero[:], 0.0).then_inc(S["zero"], 1)
    V.wait_ge(S["l_b"], 16)
    V.wait_ge(S["p4"], 1)
    V.tensor_tensor(T.en[:], T.p4[:], T.ids[:, 8:12], OP.add).then_inc(S["en"], 1)
    V.wait_ge(S["l_o"], 16)
    base(V, "A")
    V.wait_ge(S["en"], 1)
    for x in ("A", "B"):
        k = 16 * ROLES.index(x)
        V.wait_ge(S["ow" + x], 1)
        V.tensor_tensor(T["k" + x][:], T.ow[:, k:k + 4], T.en[:], OP.add).then_inc(S["kAB"], 1)
    V.wait_ge(S["owM"], 1)
    k = 16 * ROLES.index("M")
    for a in range(4):
        V.tensor_tensor(T.kM[32 * a:32 * a + 32, 0:1], T.ow[32 * a:32 * a + 32, k + a:k + a + 1],
                        T.en[32 * a:32 * a + 32, a:a + 1], OP.add).then_inc(S["kM"], 1)
    V.wait_ge(S["owS"], 1)
    V.tensor_tensor(T.rS[:], T.ow[:, 0:4], T.en[:], OP.add).then_inc(S["kS"], 1)
    V.wait_ge(S["zero"], 1)
    V.wait_ge(S["ref"], 1)
    spread(V, "S", (0, 1))
    turn("S")
    compare("S")
    quantise_onehot("S")
    for f in range(4):
        if f % 2 == 0:
            V.wait_ge(S["l_t%d" % (f // 2)], 16)
        V.quantize_mx(T.qt[:, 128 * f:128 * f + 128], T.st[:, 128 * f:128 * f + 128],
                      T.tab_s[:, 512 * f:512 * f + 512]).then_inc(S["qt%d" % f], 1)
    quantise_entry("S")
    spread(V, "A", (0, 1))
    turn("A")
    compare("A")
    turn("B")
    quantise_onehot("A")
    compare("B")
    quantise_onehot("B")
    evacuate(V, "A", (3,))
    quantise_entry("A")
    turn("M")
    compare("M")
    quantise_onehot("M")
    quantise_entry("B")
    V.wait_ge(S["l_w"], 16)
    V.quantize_mx(T.qw[:], T.sw[:], T.w_s[:]).then_inc(S["qw"], 1)
    evacuate(V, "M", (1, 3))
    quantise_entry("M")
    V.wait_ge(S["my"], 1)
    for B in range(4):
        V.tensor_copy(T.ysb[:, B:128:4], T.p0[:, 32 * B:32 * B + 32]).then_inc(S["yc"], 1)

    for x in ROLES:
        P.wait_ge(S["qo" + x], 1)
        if x == "B":
            P.wait_ge(S["evS"], 4)
        if x == "M":
            P.wait_ge(S["evA"], 4)
        for f in range(4):
            if x == "S":
                P.wait_ge(S["qt%d" % f], 1)
            P.matmul_mx(psum[x][:, 512 * f:512 * f + 128], T.qt[:, 128 * f:128 * f + 128], T.st[:, 128 * f:128 * f + 128],
                        T["qo" + x][:], T["so" + x][:], True, True).then_inc(S["mm%s%d" % (x, f)], 1)
    P.wait_ge(S["evB"], 4)
    P.wait_ge(S["qw"], 1)
    P.wait_ge(S["qeS"], 1)
    order = ("S", "A", "B", "M")
    for i, x in enumerate(order):
        if x == "S":
            c, s = T.qeS, T.seS
        else:
            P.wait_ge(S["a" + x], entries_in[x])
            c, s = T["lc" + x], T["lp" + x]
        mm = P.matmul_mx(T.p0[:, 0:128], T.qw[:], T.sw[:], c[:], s[:], i == 0, i == 3)
        if i == 3:
            mm.then_inc(S["my"], 1)
